import numpy as np
import ml_dtypes


def mxq(x, axis, fmt="e4m3"):
    dtype, down = {"e4m3": (ml_dtypes.float8_e4m3fn, 7), "e5m2": (ml_dtypes.float8_e5m2, 14)}[fmt]
    v = np.moveaxis(np.asarray(x, np.float32).astype(ml_dtypes.bfloat16).astype(np.float64), axis, -1)
    blocks = v.reshape(v.shape[:-1] + (-1, 32))
    amax = np.abs(blocks).max(-1, keepdims=True)
    byte = np.maximum(np.where(amax > 0, np.frexp(amax)[1] - 1 + 127, 0) - down, 1)
    scale = np.exp2(byte - 127.0)
    codes = (blocks / scale).astype(np.float32).astype(dtype).astype(np.float64)
    return np.moveaxis((codes * scale).reshape(v.shape), -1, axis)


WIDE = False


def mx_kscale(k):
    if not WIDE:
        return np.ones(k)
    levels = np.array([10, -10, 5, -5, 0])
    if k % 512:
        return np.exp2(np.random.permutation(np.resize(levels, k // 32))).repeat(32)
    a = np.empty((k // 512, 16))
    for p in range(k // 512):
        a[p, :8] = np.random.permutation(np.resize(levels, 8))
        for g in range(8):
            far = levels[np.abs(levels - a[p, g]) >= 10]
            a[p, g + 8] = far[np.random.randint(len(far))]
    return np.exp2(a.ravel()).repeat(32)


def f64(x):
    return np.asarray(x).astype(np.float64)


def striped(idx):
    return np.tile(idx.reshape(-1, 16).T, (8, 1)).astype(np.uint16)


def unstriped(offs):
    return offs[:16].T.reshape(-1).astype(np.int64)


E2M1 = np.array([0.0, 0.5, 1.0, 1.5, 2.0, 3.0, 4.0, 6.0, -0.0, -0.5, -1.0, -1.5, -2.0, -3.0, -4.0, -6.0])


def pack_weight(w, fmt):
    k, n = w.shape
    w = f64(np.asarray(w, np.float32).astype(ml_dtypes.bfloat16)).reshape(k // 32, 32, n)
    amax = np.abs(w).max(1)
    if fmt == "e4m3":
        byte = np.frexp(amax)[1] - 1 + 127 - 7
    else:
        mant, ex = np.frexp(amax / 6.0)
        byte = np.where(mant > 0.5, ex, ex - 1) + 127
    byte = np.clip(np.where(amax > 0, byte, 1), 1, 254)
    scaled = (w * np.exp2(127.0 - byte)[:, None, :]).reshape(k, n).astype(np.float32)
    by_word = np.ascontiguousarray(scaled.reshape(k // 512, 128, 4, n).transpose(0, 1, 3, 2))
    if fmt == "e4m3":
        words = by_word.astype(ml_dtypes.float8_e4m3fn).view(np.uint8)
    else:
        c = by_word.astype(ml_dtypes.float4_e2m1fn).view(np.uint8) & 0xF
        words = (c[..., 0::2] | (c[..., 1::2] << 4)).reshape(k // 512, 128, 2 * n)
    return np.ascontiguousarray(words), np.ascontiguousarray(byte.astype(np.uint8).reshape(k // 512, 16, n))


def unpack_weight(words, scales, fmt):
    g, _, n = scales.shape
    words = np.ascontiguousarray(words).reshape(g, 128, n, -1)
    if fmt == "e4m3":
        vals = words.view(ml_dtypes.float8_e4m3fn).astype(np.float64)
    else:
        nib = np.empty((g, 128, n, 4), np.uint8)
        nib[..., 0::2] = words & 0xF
        nib[..., 1::2] = words >> 4
        vals = E2M1[nib]
    vals = vals * np.repeat(np.exp2(scales.astype(np.float64) - 127.0), 8, axis=1)[..., None]
    return vals.transpose(0, 1, 3, 2).reshape(g * 512, n)


def silu(v):
    return v / (1.0 + np.exp(-np.maximum(v, -700.0)))


K, M, T, S = 1536, 256, 4096, 1536


def setup_inputs():
    n = np.random.standard_normal
    s = mx_kscale(K)[:, None]
    v = pack_weight(n((K, T)) * s, "e4m3")
    return {
        "tab_words": v[0],
        "tab_scales": v[1],
        "w": (n((K, M)) / np.sqrt(K) / s).astype(np.float32),
        "rT": n((M, T)).astype(np.float32),
        "b": (0.3 * n(256)).astype(np.float32),
        "offs": striped(np.random.permutation(T)[:S]),
    }


def reference(tab_words, tab_scales, w, rT, b, offs):
    tab_ = unpack_weight(tab_words, tab_scales, "e4m3")[:, unstriped(offs)]
    w_ = mxq(f64(w), 0, "e4m3")
    y = w_.T @ tab_
    return (silu(y + f64(b)[:, None])) + f64(rT)[:, unstriped(offs)]

@@ -1,0 +1,129 @@
+from contextlib import ExitStack
+
+import concourse.mybir as mybir
+
+K, M, T, S = 1536, 256, 4096, 1536
+FLOPS = 2 * K * M * S
+
+F32 = mybir.dt.float32
+BF16 = mybir.dt.bfloat16
+I32 = mybir.dt.int32
+U32 = mybir.dt.uint32
+U16 = mybir.dt.uint16
+U8 = mybir.dt.uint8
+FP8X4 = mybir.dt.float8_e4m3fn_x4
+SILU = mybir.ActivationFunctionType.Silu
+ADD = mybir.AluOpType.add
+
+P = 128
+PACK = 4
+PASSES = K // (P * PACK)
+HALVES = M // P
+CHUNK = 512
+CHUNKS = S // CHUNK
+LIST_ROWS = 16
+QUADRANTS = 4
+
+
+def tile_list_tabres_silu_kernel(tc, tab_words, tab_scales, w, rT, b, offs, out):
+    nc = tc.nc
+    with ExitStack() as ctx:
+        held = ctx.enter_context(tc.tile_pool(name="held", bufs=1))
+        psum = ctx.enter_context(tc.psum_pool(name="psum", bufs=1))
+
+        offsets = held.tile([P, S // LIST_ROWS], U16, name="offsets")
+        nc.sync.dma_start(offsets[:], offs)
+
+        def chunk_offsets(c):
+            cols = CHUNK // LIST_ROWS
+            return offsets[:, c * cols : (c + 1) * cols]
+
+        scale_rows = held.tile([P, T // 4], I32, name="scale_rows", align_bytes=64)
+        nc.vector.memset(scale_rows[:], 0)
+        for q in range(QUADRANTS):
+            nc.gpsimd.dma_start(
+                scale_rows[32 * q : 32 * q + 4 * PASSES, :],
+                tab_scales[:, 4 * q : 4 * q + 4, :].bitcast(I32),
+            )
+
+        words = [held.tile([P, T], I32, name="words%d" % a, align_bytes=64) for a in range(PASSES)]
+        resid = [held.tile([P, T], F32, name="resid%d" % h, align_bytes=64) for h in range(HALVES)]
+        w_raw = held.tile([P, PASSES, PACK, M], F32, name="w_raw", align_bytes=64)
+        bias = held.tile([P, HALVES], F32, name="bias", align_bytes=64)
+
+        def load_words(a):
+            nc.sync.dma_start(words[a][:], tab_words[a].rearrange("p t i -> p (t i)").bitcast(I32))
+
+        load_words(0)
+        nc.sync.dma_start(
+            w_raw[:].rearrange("p a j n -> p a (j n)"),
+            w.rearrange("(a p j) n -> p a (j n)", a=PASSES, j=PACK),
+        )
+        load_words(1)
+        load_words(2)
+        for h in range(HALVES):
+            nc.sync.dma_start(resid[h][:], rT[h * P : (h + 1) * P, :])
+        with nc.allow_non_contiguous_dma(reason="one bias value a partition"):
+            nc.scalar.dma_start(bias[:], b.rearrange("(h p) -> p h", p=P))
+
+        picked = [held.tile([P, S], U32, name="picked%d" % a, align_bytes=64) for a in range(PASSES)]
+        picked_scales = held.tile([P, S], U8, name="picked_scales", align_bytes=64)
+        w_bf = [held.tile([P, M, PACK], BF16, name="w_bf%d" % a, align_bytes=64) for a in range(PASSES)]
+        w_codes = [held.tile([P, M], U32, name="w_codes%d" % a, align_bytes=64) for a in range(PASSES)]
+        w_scales = [held.tile([P, M], U8, name="w_scales%d" % a, align_bytes=64) for a in range(PASSES)]
+        acc = [[psum.tile([P, CHUNK], F32, name="acc%d_%d" % (h, c)) for c in range(CHUNKS)] for h in range(HALVES)]
+
+        def gather_words(a):
+            nc.vector.tensor_copy(picked[a][:], words[a][:].bitcast(U32).indirect(offsets[:]))
+
+        def multiply(a):
+            for h in range(HALVES):
+                for c in range(CHUNKS):
+                    n_cols = slice(h * P, (h + 1) * P)
+                    j_cols = slice(c * CHUNK, (c + 1) * CHUNK)
+                    nc.tensor.matmul_mx(
+                        out=acc[h][c][:],
+                        lhsT=w_codes[a][:, n_cols].bitcast(FP8X4),
+                        lhsT_scale=w_scales[a][:, n_cols],
+                        rhs=picked[a][:, j_cols].bitcast(FP8X4),
+                        rhs_scale=picked_scales[4 * a : P, j_cols],
+                        start=(a == 0),
+                        stop=(a == PASSES - 1),
+                    )
+
+        gather_words(0)
+        nc.vector.tensor_copy(picked_scales[:], scale_rows[:].bitcast(U8).indirect(offsets[:]))
+        for a in range(PASSES):
+            nc.scalar.copy(w_bf[a][:], w_raw[:, a].rearrange("p j n -> p n j"))
+        for a in range(PASSES):
+            nc.vector.quantize_mx(
+                out=w_codes[a][:].bitcast(FP8X4),
+                scales=w_scales[a][:],
+                in_=w_bf[a][:].rearrange("p n j -> p (n j)"),
+            )
+        multiply(0)
+        gather_words(1)
+        multiply(1)
+        gather_words(2)
+        multiply(2)
+
+        act = [[held.tile([P, CHUNK], F32, name="act%d_%d" % (h, c), align_bytes=64) for c in range(CHUNKS)] for h in range(HALVES)]
+        res = [[held.tile([P, CHUNK], F32, name="res%d_%d" % (h, c), align_bytes=64) for c in range(CHUNKS)] for h in range(HALVES)]
+        done = [[held.tile([P, CHUNK], F32, name="done%d_%d" % (h, c), align_bytes=64) for c in range(CHUNKS)] for h in range(HALVES)]
+        for h in range(HALVES):
+            for c in range(CHUNKS):
+                nc.scalar.activation(act[h][c][:], acc[h][c][:], SILU, bias=bias[:, h : h + 1])
+
+        def gather_resid(h, c):
+            nc.vector.tensor_copy(res[h][c][:], resid[h][:].indirect(chunk_offsets(c)))
+
+        def finish(h, c):
+            nc.vector.tensor_tensor(done[h][c][:], act[h][c][:], res[h][c][:], ADD)
+            nc.sync.dma_start(out[h * P : (h + 1) * P, c * CHUNK : (c + 1) * CHUNK], done[h][c][:])
+
+        for h in range(HALVES):
+            gather_resid(h, 0)
+            for c in range(1, CHUNKS):
+                gather_resid(h, c)
+                finish(h, c - 1)
+            finish(h, CHUNKS - 1)

@@ -118,8 +118,15 @@ def tile_list_tabres_silu_kernel(tc, tab_words, tab_scales, w, rT, b, offs, out)
             nc.vector.tensor_copy(res[h][c][:], resid[h][:].indirect(chunk_offsets(c)))
 
         def finish(h, c):
-            nc.vector.tensor_tensor(done[h][c][:], act[h][c][:], res[h][c][:], ADD)
-            nc.sync.dma_start(out[h * P : (h + 1) * P, c * CHUNK : (c + 1) * CHUNK], done[h][c][:])
+            last = (h, c) == (HALVES - 1, CHUNKS - 1)
+            adder = nc.vector if last else nc.gpsimd
+            pieces = 2 if last else 1
+            width = CHUNK // pieces
+            for i in range(pieces):
+                cols = slice(i * width, (i + 1) * width)
+                adder.tensor_tensor(done[h][c][:, cols], act[h][c][:, cols], res[h][c][:, cols], ADD)
+                j0 = c * CHUNK + i * width
+                nc.sync.dma_start(out[h * P : (h + 1) * P, j0 : j0 + width], done[h][c][:, cols])
 
         for h in range(HALVES):
             gather_resid(h, 0)

@@ -23,6 +23,7 @@ CHUNK = 512
 CHUNKS = S // CHUNK
 LIST_ROWS = 16
 QUADRANTS = 4
+SHARED_SPLIT = 384
 
 
 def tile_list_tabres_silu_kernel(tc, tab_words, tab_scales, w, rT, b, offs, out):
@@ -49,7 +50,8 @@ def tile_list_tabres_silu_kernel(tc, tab_words, tab_scales, w, rT, b, offs, out)
         words = [held.tile([P, T], I32, name="words%d" % a, align_bytes=64) for a in range(PASSES)]
         resid = [held.tile([P, T], F32, name="resid%d" % h, align_bytes=64) for h in range(HALVES)]
         w_raw = held.tile([P, PASSES, PACK, M], F32, name="w_raw", align_bytes=64)
-        bias = held.tile([P, HALVES], F32, name="bias", align_bytes=64)
+        bias_rows = held.tile([P, P], F32, name="bias_rows", align_bytes=64)
+        bias = held.tile([P, P], F32, name="bias", align_bytes=64)
 
         def load_words(a):
             nc.sync.dma_start(words[a][:], tab_words[a].rearrange("p t i -> p (t i)").bitcast(I32))
@@ -63,8 +65,12 @@ def tile_list_tabres_silu_kernel(tc, tab_words, tab_scales, w, rT, b, offs, out)
         load_words(2)
         for h in range(HALVES):
             nc.sync.dma_start(resid[h][:], rT[h * P : (h + 1) * P, :])
-        with nc.allow_non_contiguous_dma(reason="one bias value a partition"):
-            nc.scalar.dma_start(bias[:], b.rearrange("(h p) -> p h", p=P))
+        nc.vector.memset(bias_rows[:], 0.0)
+        nc.scalar.dma_start(
+            bias_rows[0:P:32, 0 : HALVES * 32].rearrange("q (h i) -> q h i", h=HALVES),
+            b.rearrange("(h q i) -> q h i", h=HALVES, q=QUADRANTS),
+        )
+        nc.vector.transpose(bias[:], bias_rows[:])
 
         picked = [held.tile([P, S], U32, name="picked%d" % a, align_bytes=64) for a in range(PASSES)]
         picked_scales = held.tile([P, S], U8, name="picked_scales", align_bytes=64)
@@ -112,25 +118,31 @@ def tile_list_tabres_silu_kernel(tc, tab_words, tab_scales, w, rT, b, offs, out)
         done = [[held.tile([P, CHUNK], F32, name="done%d_%d" % (h, c), align_bytes=64) for c in range(CHUNKS)] for h in range(HALVES)]
         for h in range(HALVES):
             for c in range(CHUNKS):
-                nc.scalar.activation(act[h][c][:], acc[h][c][:], SILU, bias=bias[:, h : h + 1])
+                nc.scalar.activation(act[h][c][:], acc[h][c][:], SILU, bias=bias[:, 32 * h : 32 * h + 1])
 
         def gather_resid(h, c):
             nc.vector.tensor_copy(res[h][c][:], resid[h][:].indirect(chunk_offsets(c)))
 
-        def finish(h, c):
-            last = (h, c) == (HALVES - 1, CHUNKS - 1)
-            adder = nc.vector if last else nc.gpsimd
-            pieces = 2 if last else 1
-            width = CHUNK // pieces
-            for i in range(pieces):
-                cols = slice(i * width, (i + 1) * width)
-                adder.tensor_tensor(done[h][c][:, cols], act[h][c][:, cols], res[h][c][:, cols], ADD)
-                j0 = c * CHUNK + i * width
-                nc.sync.dma_start(out[h * P : (h + 1) * P, j0 : j0 + width], done[h][c][:, cols])
+        def add(engine, h, c, cols):
+            engine.tensor_tensor(done[h][c][:, cols], act[h][c][:, cols], res[h][c][:, cols], ADD)
 
-        for h in range(HALVES):
-            gather_resid(h, 0)
-            for c in range(1, CHUNKS):
-                gather_resid(h, c)
-                finish(h, c - 1)
-            finish(h, CHUNKS - 1)
+        def store(h, c, cols):
+            j0 = c * CHUNK
+            nc.sync.dma_start(out[h * P : (h + 1) * P, j0 + cols.start : j0 + cols.stop], done[h][c][:, cols])
+
+        whole = slice(0, CHUNK)
+        for c in range(CHUNKS):
+            gather_resid(0, c)
+            add(nc.gpsimd, 0, c, whole)
+            store(0, c, whole)
+        gather_resid(1, 0)
+        add(nc.gpsimd, 1, 0, whole)
+        store(1, 0, whole)
+        gather_resid(1, 1)
+        add(nc.gpsimd, 1, 1, slice(0, SHARED_SPLIT))
+        gather_resid(1, 2)
+        add(nc.vector, 1, 1, slice(SHARED_SPLIT, CHUNK))
+        store(1, 1, whole)
+        for cols in (slice(0, CHUNK // 2), slice(CHUNK // 2, CHUNK)):
+            add(nc.vector, 1, 2, cols)
+            store(1, 2, cols)

@@ -23,7 +23,6 @@ CHUNK = 512
 CHUNKS = S // CHUNK
 LIST_ROWS = 16
 QUADRANTS = 4
-SHARED_SPLIT = 384
 
 
 def tile_list_tabres_silu_kernel(tc, tab_words, tab_scales, w, rT, b, offs, out):
@@ -34,10 +33,6 @@ def tile_list_tabres_silu_kernel(tc, tab_words, tab_scales, w, rT, b, offs, out)
 
         offsets = held.tile([P, S // LIST_ROWS], U16, name="offsets")
         nc.sync.dma_start(offsets[:], offs)
-
-        def chunk_offsets(c):
-            cols = CHUNK // LIST_ROWS
-            return offsets[:, c * cols : (c + 1) * cols]
 
         scale_rows = held.tile([P, T // 4], I32, name="scale_rows", align_bytes=64)
         nc.vector.memset(scale_rows[:], 0)
@@ -114,35 +109,20 @@ def tile_list_tabres_silu_kernel(tc, tab_words, tab_scales, w, rT, b, offs, out)
         multiply(2)
 
         act = [[held.tile([P, CHUNK], F32, name="act%d_%d" % (h, c), align_bytes=64) for c in range(CHUNKS)] for h in range(HALVES)]
-        res = [[held.tile([P, CHUNK], F32, name="res%d_%d" % (h, c), align_bytes=64) for c in range(CHUNKS)] for h in range(HALVES)]
         done = [[held.tile([P, CHUNK], F32, name="done%d_%d" % (h, c), align_bytes=64) for c in range(CHUNKS)] for h in range(HALVES)]
         for h in range(HALVES):
             for c in range(CHUNKS):
                 nc.scalar.activation(act[h][c][:], acc[h][c][:], SILU, bias=bias[:, 32 * h : 32 * h + 1])
 
-        def gather_resid(h, c):
-            nc.vector.tensor_copy(res[h][c][:], resid[h][:].indirect(chunk_offsets(c)))
-
-        def add(engine, h, c, cols):
-            engine.tensor_tensor(done[h][c][:, cols], act[h][c][:, cols], res[h][c][:, cols], ADD)
-
-        def store(h, c, cols):
+        def add_resid_and_store(h, c, cols):
             j0 = c * CHUNK
+            listed = offsets[:, (j0 + cols.start) // LIST_ROWS : (j0 + cols.stop) // LIST_ROWS]
+            nc.vector.tensor_tensor(done[h][c][:, cols], resid[h][:].indirect(listed), act[h][c][:, cols], ADD)
             nc.sync.dma_start(out[h * P : (h + 1) * P, j0 + cols.start : j0 + cols.stop], done[h][c][:, cols])
 
         whole = slice(0, CHUNK)
-        for c in range(CHUNKS):
-            gather_resid(0, c)
-            add(nc.gpsimd, 0, c, whole)
-            store(0, c, whole)
-        gather_resid(1, 0)
-        add(nc.gpsimd, 1, 0, whole)
-        store(1, 0, whole)
-        gather_resid(1, 1)
-        add(nc.gpsimd, 1, 1, slice(0, SHARED_SPLIT))
-        gather_resid(1, 2)
-        add(nc.vector, 1, 1, slice(SHARED_SPLIT, CHUNK))
-        store(1, 1, whole)
-        for cols in (slice(0, CHUNK // 2), slice(CHUNK // 2, CHUNK)):
-            add(nc.vector, 1, 2, cols)
-            store(1, 2, cols)
+        for h in range(HALVES):
+            for c in range(CHUNKS):
+                last = h == HALVES - 1 and c == CHUNKS - 1
+                for cols in (slice(0, CHUNK // 2), slice(CHUNK // 2, CHUNK)) if last else (whole,):
+                    add_resid_and_store(h, c, cols)

@@ -74,25 +74,27 @@ def tile_list_tabres_silu_kernel(tc, tab_words, tab_scales, w, rT, b, offs, out)
         w_scales = [held.tile([P, M], U8, name="w_scales%d" % a, align_bytes=64) for a in range(PASSES)]
         acc = [[psum.tile([P, CHUNK], F32, name="acc%d_%d" % (h, c)) for c in range(CHUNKS)] for h in range(HALVES)]
 
-        def gather_words(a):
-            nc.vector.tensor_copy(picked[a][:], words[a][:].bitcast(U32).indirect(offsets[:]))
+        def gather_words(a, first, count):
+            nc.vector.tensor_copy(
+                picked[a][:, first : first + count],
+                words[a][:].bitcast(U32).indirect(offsets[:, first // LIST_ROWS : (first + count) // LIST_ROWS]),
+            )
 
-        def multiply(a):
+        def multiply(a, c):
+            j_cols = slice(c * CHUNK, (c + 1) * CHUNK)
             for h in range(HALVES):
-                for c in range(CHUNKS):
-                    n_cols = slice(h * P, (h + 1) * P)
-                    j_cols = slice(c * CHUNK, (c + 1) * CHUNK)
-                    nc.tensor.matmul_mx(
-                        out=acc[h][c][:],
-                        lhsT=w_codes[a][:, n_cols].bitcast(FP8X4),
-                        lhsT_scale=w_scales[a][:, n_cols],
-                        rhs=picked[a][:, j_cols].bitcast(FP8X4),
-                        rhs_scale=picked_scales[4 * a : P, j_cols],
-                        start=(a == 0),
-                        stop=(a == PASSES - 1),
-                    )
+                n_cols = slice(h * P, (h + 1) * P)
+                nc.tensor.matmul_mx(
+                    out=acc[h][c][:],
+                    lhsT=w_codes[a][:, n_cols].bitcast(FP8X4),
+                    lhsT_scale=w_scales[a][:, n_cols],
+                    rhs=picked[a][:, j_cols].bitcast(FP8X4),
+                    rhs_scale=picked_scales[4 * a : P, j_cols],
+                    start=(a == 0),
+                    stop=(a == PASSES - 1),
+                )
 
-        gather_words(0)
+        gather_words(0, 0, S)
         nc.vector.tensor_copy(picked_scales[:], scale_rows[:].bitcast(U8).indirect(offsets[:]))
         for a in range(PASSES):
             nc.scalar.copy(w_bf[a][:], w_raw[:, a].rearrange("p j n -> p n j"))
@@ -102,11 +104,14 @@ def tile_list_tabres_silu_kernel(tc, tab_words, tab_scales, w, rT, b, offs, out)
                 scales=w_scales[a][:],
                 in_=w_bf[a][:].rearrange("p n j -> p (n j)"),
             )
-        multiply(0)
-        gather_words(1)
-        multiply(1)
-        gather_words(2)
-        multiply(2)
+        for c in range(CHUNKS):
+            multiply(0, c)
+        gather_words(1, 0, S)
+        for c in range(CHUNKS):
+            multiply(1, c)
+        for c in range(CHUNKS):
+            gather_words(2, c * CHUNK, CHUNK)
+            multiply(2, c)
 
         act = [[held.tile([P, CHUNK], F32, name="act%d_%d" % (h, c), align_bytes=64) for c in range(CHUNKS)] for h in range(HALVES)]
         done = [[held.tile([P, CHUNK], F32, name="done%d_%d" % (h, c), align_bytes=64) for c in range(CHUNKS)] for h in range(HALVES)]

@@ -34,7 +34,7 @@ def tile_list_tabres_silu_kernel(tc, tab_words, tab_scales, w, rT, b, offs, out)
         offsets = held.tile([P, S // LIST_ROWS], U16, name="offsets")
         nc.sync.dma_start(offsets[:], offs)
 
-        scale_rows = held.tile([P, T // 4], I32, name="scale_rows", align_bytes=64)
+        scale_rows = held.tile([P, T // 4], I32, name="scale_rows", align_bytes=256)
         nc.vector.memset(scale_rows[:], 0)
         for q in range(QUADRANTS):
             nc.gpsimd.dma_start(
@@ -42,11 +42,11 @@ def tile_list_tabres_silu_kernel(tc, tab_words, tab_scales, w, rT, b, offs, out)
                 tab_scales[:, 4 * q : 4 * q + 4, :].bitcast(I32),
             )
 
-        words = [held.tile([P, T], I32, name="words%d" % a, align_bytes=64) for a in range(PASSES)]
-        resid = [held.tile([P, T], F32, name="resid%d" % h, align_bytes=64) for h in range(HALVES)]
-        w_raw = held.tile([P, PASSES, PACK, M], F32, name="w_raw", align_bytes=64)
-        bias_rows = held.tile([P, P], F32, name="bias_rows", align_bytes=64)
-        bias = held.tile([P, P], F32, name="bias", align_bytes=64)
+        words = [held.tile([P, T], I32, name="words%d" % a, align_bytes=256) for a in range(PASSES)]
+        resid = [held.tile([P, T], F32, name="resid%d" % h, align_bytes=256) for h in range(HALVES)]
+        w_raw = held.tile([P, PASSES, PACK, M], F32, name="w_raw", align_bytes=256)
+        bias_rows = held.tile([P, P], F32, name="bias_rows", align_bytes=256)
+        bias = held.tile([P, P], F32, name="bias", align_bytes=256)
 
         def load_words(a):
             nc.sync.dma_start(words[a][:], tab_words[a].rearrange("p t i -> p (t i)").bitcast(I32))
@@ -66,12 +66,14 @@ def tile_list_tabres_silu_kernel(tc, tab_words, tab_scales, w, rT, b, offs, out)
             b.rearrange("(h q i) -> q h i", h=HALVES, q=QUADRANTS),
         )
         nc.vector.transpose(bias[:], bias_rows[:])
+        warm = held.tile([P, 1], F32, name="warm")
+        nc.scalar.activation(warm[:], bias_rows[:, P - 1 : P], SILU)
 
-        picked = [held.tile([P, S], U32, name="picked%d" % a, align_bytes=64) for a in range(PASSES)]
-        picked_scales = held.tile([P, S], U8, name="picked_scales", align_bytes=64)
-        w_bf = [held.tile([P, M, PACK], BF16, name="w_bf%d" % a, align_bytes=64) for a in range(PASSES)]
-        w_codes = [held.tile([P, M], U32, name="w_codes%d" % a, align_bytes=64) for a in range(PASSES)]
-        w_scales = [held.tile([P, M], U8, name="w_scales%d" % a, align_bytes=64) for a in range(PASSES)]
+        picked = [held.tile([P, S], U32, name="picked%d" % a, align_bytes=256) for a in range(PASSES)]
+        picked_scales = held.tile([P, S], U8, name="picked_scales", align_bytes=256)
+        w_bf = [held.tile([P, M, PACK], BF16, name="w_bf%d" % a, align_bytes=256) for a in range(PASSES)]
+        w_codes = [held.tile([P, M], U32, name="w_codes%d" % a, align_bytes=256) for a in range(PASSES)]
+        w_scales = [held.tile([P, M], U8, name="w_scales%d" % a, align_bytes=256) for a in range(PASSES)]
         acc = [[psum.tile([P, CHUNK], F32, name="acc%d_%d" % (h, c)) for c in range(CHUNKS)] for h in range(HALVES)]
 
         def gather_words(a, first, count):
@@ -113,8 +115,8 @@ def tile_list_tabres_silu_kernel(tc, tab_words, tab_scales, w, rT, b, offs, out)
             gather_words(2, c * CHUNK, CHUNK)
             multiply(2, c)
 
-        act = [[held.tile([P, CHUNK], F32, name="act%d_%d" % (h, c), align_bytes=64) for c in range(CHUNKS)] for h in range(HALVES)]
-        done = [[held.tile([P, CHUNK], F32, name="done%d_%d" % (h, c), align_bytes=64) for c in range(CHUNKS)] for h in range(HALVES)]
+        act = [[held.tile([P, CHUNK], F32, name="act%d_%d" % (h, c), align_bytes=256) for c in range(CHUNKS)] for h in range(HALVES)]
+        done = [[held.tile([P, CHUNK], F32, name="done%d_%d" % (h, c), align_bytes=256) for c in range(CHUNKS)] for h in range(HALVES)]
         for h in range(HALVES):
             for c in range(CHUNKS):
                 nc.scalar.activation(act[h][c][:], acc[h][c][:], SILU, bias=bias[:, 32 * h : 32 * h + 1])

@@ -32,7 +32,6 @@ def tile_list_tabres_silu_kernel(tc, tab_words, tab_scales, w, rT, b, offs, out)
         psum = ctx.enter_context(tc.psum_pool(name="psum", bufs=1))
 
         offsets = held.tile([P, S // LIST_ROWS], U16, name="offsets")
-        nc.sync.dma_start(offsets[:], offs)
 
         scale_rows = held.tile([P, T // 4], I32, name="scale_rows", align_bytes=256)
         nc.vector.memset(scale_rows[:], 0)
@@ -52,6 +51,7 @@ def tile_list_tabres_silu_kernel(tc, tab_words, tab_scales, w, rT, b, offs, out)
             nc.sync.dma_start(words[a][:], tab_words[a].rearrange("p t i -> p (t i)").bitcast(I32))
 
         load_words(0)
+        nc.sync.dma_start(offsets[:], offs)
         nc.sync.dma_start(
             w_raw[:].rearrange("p a j n -> p a (j n)"),
             w.rearrange("(a p j) n -> p a (j n)", a=PASSES, j=PACK),
@@ -66,8 +66,6 @@ def tile_list_tabres_silu_kernel(tc, tab_words, tab_scales, w, rT, b, offs, out)
             b.rearrange("(h q i) -> q h i", h=HALVES, q=QUADRANTS),
         )
         nc.vector.transpose(bias[:], bias_rows[:])
-        warm = held.tile([P, 1], F32, name="warm")
-        nc.scalar.activation(warm[:], bias_rows[:, P - 1 : P], SILU)
 
         picked = [held.tile([P, S], U32, name="picked%d" % a, align_bytes=256) for a in range(PASSES)]
         picked_scales = held.tile([P, S], U8, name="picked_scales", align_bytes=256)
@@ -131,5 +129,5 @@ def tile_list_tabres_silu_kernel(tc, tab_words, tab_scales, w, rT, b, offs, out)
         for h in range(HALVES):
             for c in range(CHUNKS):
                 last = h == HALVES - 1 and c == CHUNKS - 1
-                for cols in (slice(0, CHUNK // 2), slice(CHUNK // 2, CHUNK)) if last else (whole,):
+                for cols in (slice(0, CHUNK - P), slice(CHUNK - P, CHUNK)) if last else (whole,):
                     add_resid_and_store(h, c, cols)

@@ -36,16 +36,16 @@ def tile_list_tabres_silu_kernel(tc, tab_words, tab_scales, w, rT, b, offs, out)
         scale_rows = held.tile([P, T // 4], I32, name="scale_rows", align_bytes=256)
         nc.vector.memset(scale_rows[:], 0)
         for q in range(QUADRANTS):
-            nc.gpsimd.dma_start(
+            queue = nc.scalar if q == 0 else nc.gpsimd
+            queue.dma_start(
                 scale_rows[32 * q : 32 * q + 4 * PASSES, :],
                 tab_scales[:, 4 * q : 4 * q + 4, :].bitcast(I32),
             )
 
-        words = [held.tile([P, T], I32, name="words%d" % a, align_bytes=256) for a in range(PASSES)]
+        words = [held.tile([P, T], I32, name="words%d" % a, tag="words%d" % a, align_bytes=256) for a in range(PASSES)]
         resid = [held.tile([P, T], F32, name="resid%d" % h, align_bytes=256) for h in range(HALVES)]
         w_raw = held.tile([P, PASSES, PACK, M], F32, name="w_raw", align_bytes=256)
         bias_rows = held.tile([P, P], F32, name="bias_rows", align_bytes=256)
-        bias = held.tile([P, P], F32, name="bias", align_bytes=256)
 
         def load_words(a):
             nc.sync.dma_start(words[a][:], tab_words[a].rearrange("p t i -> p (t i)").bitcast(I32))
@@ -65,7 +65,6 @@ def tile_list_tabres_silu_kernel(tc, tab_words, tab_scales, w, rT, b, offs, out)
             bias_rows[0:P:32, 0 : HALVES * 32].rearrange("q (h i) -> q h i", h=HALVES),
             b.rearrange("(h q i) -> q h i", h=HALVES, q=QUADRANTS),
         )
-        nc.vector.transpose(bias[:], bias_rows[:])
 
         picked = [held.tile([P, S], U32, name="picked%d" % a, align_bytes=256) for a in range(PASSES)]
         picked_scales = held.tile([P, S], U8, name="picked_scales", align_bytes=256)
@@ -107,6 +106,8 @@ def tile_list_tabres_silu_kernel(tc, tab_words, tab_scales, w, rT, b, offs, out)
         for c in range(CHUNKS):
             multiply(0, c)
         gather_words(1, 0, S)
+        bias = held.tile([P, P], F32, name="bias", tag="words1", align_bytes=256)
+        nc.vector.transpose(bias[:], bias_rows[:])
         for c in range(CHUNKS):
             multiply(1, c)
         for c in range(CHUNKS):

@@ -23,6 +23,7 @@ CHUNK = 512
 CHUNKS = S // CHUNK
 LIST_ROWS = 16
 QUADRANTS = 4
+PIECES = ((512, 512, 512), (640, 512, 256, 128))
 
 
 def tile_list_tabres_silu_kernel(tc, tab_words, tab_scales, w, rT, b, offs, out):
@@ -114,21 +115,17 @@ def tile_list_tabres_silu_kernel(tc, tab_words, tab_scales, w, rT, b, offs, out)
             gather_words(2, c * CHUNK, CHUNK)
             multiply(2, c)
 
-        act = [[held.tile([P, CHUNK], F32, name="act%d_%d" % (h, c), align_bytes=256) for c in range(CHUNKS)] for h in range(HALVES)]
-        done = [[held.tile([P, CHUNK], F32, name="done%d_%d" % (h, c), align_bytes=256) for c in range(CHUNKS)] for h in range(HALVES)]
+        act = [held.tile([P, S], F32, name="act%d" % h, align_bytes=256) for h in range(HALVES)]
+        done = [held.tile([P, S], F32, name="done%d" % h, align_bytes=256) for h in range(HALVES)]
         for h in range(HALVES):
             for c in range(CHUNKS):
-                nc.scalar.activation(act[h][c][:], acc[h][c][:], SILU, bias=bias[:, 32 * h : 32 * h + 1])
+                nc.scalar.activation(act[h][:, c * CHUNK : (c + 1) * CHUNK], acc[h][c][:], SILU, bias=bias[:, 32 * h : 32 * h + 1])
 
-        def add_resid_and_store(h, c, cols):
-            j0 = c * CHUNK
-            listed = offsets[:, (j0 + cols.start) // LIST_ROWS : (j0 + cols.stop) // LIST_ROWS]
-            nc.vector.tensor_tensor(done[h][c][:, cols], resid[h][:].indirect(listed), act[h][c][:, cols], ADD)
-            nc.sync.dma_start(out[h * P : (h + 1) * P, j0 + cols.start : j0 + cols.stop], done[h][c][:, cols])
-
-        whole = slice(0, CHUNK)
         for h in range(HALVES):
-            for c in range(CHUNKS):
-                last = h == HALVES - 1 and c == CHUNKS - 1
-                for cols in (slice(0, CHUNK - P), slice(CHUNK - P, CHUNK)) if last else (whole,):
-                    add_resid_and_store(h, c, cols)
+            first = 0
+            for count in PIECES[h]:
+                cols = slice(first, first + count)
+                listed = offsets[:, cols.start // LIST_ROWS : cols.stop // LIST_ROWS]
+                nc.vector.tensor_tensor(done[h][:, cols], resid[h][:].indirect(listed), act[h][:, cols], ADD)
+                nc.sync.dma_start(out[h * P : (h + 1) * P, cols], done[h][:, cols])
+                first = cols.stop

@@ -23,7 +23,7 @@ CHUNK = 512
 CHUNKS = S // CHUNK
 LIST_ROWS = 16
 QUADRANTS = 4
-PIECES = ((512, 512, 512), (640, 512, 256, 128))
+PIECES = ((512, 512, 512), (704, 448, 256, 128))
 
 
 def tile_list_tabres_silu_kernel(tc, tab_words, tab_scales, w, rT, b, offs, out):

@@ -24,6 +24,7 @@ CHUNKS = S // CHUNK
 LIST_ROWS = 16
 QUADRANTS = 4
 PIECES = ((512, 512, 512), (704, 448, 256, 128))
+SHORT_ROW_BYTES = 4096
 
 
 def tile_list_tabres_silu_kernel(tc, tab_words, tab_scales, w, rT, b, offs, out):
@@ -32,100 +33,91 @@ def tile_list_tabres_silu_kernel(tc, tab_words, tab_scales, w, rT, b, offs, out)
         held = ctx.enter_context(tc.tile_pool(name="held", bufs=1))
         psum = ctx.enter_context(tc.psum_pool(name="psum", bufs=1))
 
-        offsets = held.tile([P, S // LIST_ROWS], U16, name="offsets")
+        def sbuf(name, shape, dtype, tag=None):
+            return held.tile(shape, dtype, name=name, tag=tag or name, align_bytes=256)
 
-        scale_rows = held.tile([P, T // 4], I32, name="scale_rows", align_bytes=256)
+        def listed(first, count):
+            return offsets[:, first // LIST_ROWS : (first + count) // LIST_ROWS]
+
+        offsets = held.tile([P, S // LIST_ROWS], U16, name="offsets")
+        scale_rows = sbuf("scale_rows", [P, T // 4], I32, tag="first_gather")
+        bias_rows = sbuf("bias_rows", [P, P], F32)
+        w_raw = sbuf("w_raw", [P, PASSES, PACK, M], F32)
+        words = [sbuf("words%d" % a, [P, T], I32) for a in range(PASSES)]
+        resid = [sbuf("resid%d" % h, [P, T], F32) for h in range(HALVES)]
+
         nc.vector.memset(scale_rows[:], 0)
+        nc.vector.memset(bias_rows[:], 0.0)
         for q in range(QUADRANTS):
             queue = nc.scalar if q == 0 else nc.gpsimd
             queue.dma_start(
                 scale_rows[32 * q : 32 * q + 4 * PASSES, :],
                 tab_scales[:, 4 * q : 4 * q + 4, :].bitcast(I32),
             )
-
-        words = [held.tile([P, T], I32, name="words%d" % a, tag="words%d" % a, align_bytes=256) for a in range(PASSES)]
-        resid = [held.tile([P, T], F32, name="resid%d" % h, align_bytes=256) for h in range(HALVES)]
-        w_raw = held.tile([P, PASSES, PACK, M], F32, name="w_raw", align_bytes=256)
-        bias_rows = held.tile([P, P], F32, name="bias_rows", align_bytes=256)
-
-        def load_words(a):
-            nc.sync.dma_start(words[a][:], tab_words[a].rearrange("p t i -> p (t i)").bitcast(I32))
-
-        load_words(0)
-        nc.sync.dma_start(offsets[:], offs)
-        nc.sync.dma_start(
-            w_raw[:].rearrange("p a j n -> p a (j n)"),
-            w.rearrange("(a p j) n -> p a (j n)", a=PASSES, j=PACK),
-        )
-        load_words(1)
-        load_words(2)
-        for h in range(HALVES):
-            nc.sync.dma_start(resid[h][:], rT[h * P : (h + 1) * P, :])
-        nc.vector.memset(bias_rows[:], 0.0)
         nc.scalar.dma_start(
             bias_rows[0:P:32, 0 : HALVES * 32].rearrange("q (h i) -> q h i", h=HALVES),
             b.rearrange("(h q i) -> q h i", h=HALVES, q=QUADRANTS),
         )
 
-        picked = [held.tile([P, S], U32, name="picked%d" % a, align_bytes=256) for a in range(PASSES)]
-        picked_scales = held.tile([P, S], U8, name="picked_scales", align_bytes=256)
-        w_bf = [held.tile([P, M, PACK], BF16, name="w_bf%d" % a, align_bytes=256) for a in range(PASSES)]
-        w_codes = [held.tile([P, M], U32, name="w_codes%d" % a, align_bytes=256) for a in range(PASSES)]
-        w_scales = [held.tile([P, M], U8, name="w_scales%d" % a, align_bytes=256) for a in range(PASSES)]
-        acc = [[psum.tile([P, CHUNK], F32, name="acc%d_%d" % (h, c)) for c in range(CHUNKS)] for h in range(HALVES)]
+        nc.sync.dma_start(offsets[:], offs)
+        nc.sync.dma_start(
+            w_raw[:].rearrange("p a j n -> p a (j n)"),
+            w.rearrange("(a p j) n -> p a (j n)", a=PASSES, j=PACK),
+        )
+        for a in range(PASSES):
+            rows = tab_words[a].rearrange("p t i -> p (t i)").bitcast(I32)
+            nc.sync.dma_start(words[a][:], rows, max_dma_last_dim=SHORT_ROW_BYTES if a == 0 else None)
+        for h in range(HALVES):
+            nc.sync.dma_start(resid[h][:], rT[h * P : (h + 1) * P, :])
 
-        def gather_words(a, first, count):
-            nc.vector.tensor_copy(
-                picked[a][:, first : first + count],
-                words[a][:].bitcast(U32).indirect(offsets[:, first // LIST_ROWS : (first + count) // LIST_ROWS]),
-            )
-
-        def multiply(a, c):
-            j_cols = slice(c * CHUNK, (c + 1) * CHUNK)
-            for h in range(HALVES):
-                n_cols = slice(h * P, (h + 1) * P)
-                nc.tensor.matmul_mx(
-                    out=acc[h][c][:],
-                    lhsT=w_codes[a][:, n_cols].bitcast(FP8X4),
-                    lhsT_scale=w_scales[a][:, n_cols],
-                    rhs=picked[a][:, j_cols].bitcast(FP8X4),
-                    rhs_scale=picked_scales[4 * a : P, j_cols],
-                    start=(a == 0),
-                    stop=(a == PASSES - 1),
-                )
-
-        gather_words(0, 0, S)
+        picked_scales = sbuf("picked_scales", [P, S], U8)
         nc.vector.tensor_copy(picked_scales[:], scale_rows[:].bitcast(U8).indirect(offsets[:]))
+        bias = sbuf("bias", [P, P], F32)
+        nc.vector.transpose(bias[:], bias_rows[:])
+
+        w_codes, w_scales = [], []
         for a in range(PASSES):
-            nc.scalar.copy(w_bf[a][:], w_raw[:, a].rearrange("p j n -> p n j"))
-        for a in range(PASSES):
+            rounded = sbuf("w_bf%d" % a, [P, M, PACK], BF16)
+            nc.scalar.copy(rounded[:], w_raw[:, a].rearrange("p j n -> p n j"))
+            w_codes.append(sbuf("w_codes%d" % a, [P, M], U32))
+            w_scales.append(sbuf("w_scales%d" % a, [P, M], U8))
             nc.vector.quantize_mx(
                 out=w_codes[a][:].bitcast(FP8X4),
                 scales=w_scales[a][:],
-                in_=w_bf[a][:].rearrange("p n j -> p (n j)"),
+                in_=rounded[:].rearrange("p n j -> p (n j)"),
             )
-        for c in range(CHUNKS):
-            multiply(0, c)
-        gather_words(1, 0, S)
-        bias = held.tile([P, P], F32, name="bias", tag="words1", align_bytes=256)
-        nc.vector.transpose(bias[:], bias_rows[:])
-        for c in range(CHUNKS):
-            multiply(1, c)
-        for c in range(CHUNKS):
-            gather_words(2, c * CHUNK, CHUNK)
-            multiply(2, c)
 
-        act = [held.tile([P, S], F32, name="act%d" % h, align_bytes=256) for h in range(HALVES)]
-        done = [held.tile([P, S], F32, name="done%d" % h, align_bytes=256) for h in range(HALVES)]
-        for h in range(HALVES):
+        acc = [[psum.tile([P, CHUNK], F32, name="acc%d_%d" % (h, c)) for c in range(CHUNKS)] for h in range(HALVES)]
+        for a in range(PASSES):
+            picked = sbuf("picked%d" % a, [P, S], U32, tag="first_gather" if a == 0 else None)
+            step = CHUNK if a == PASSES - 1 else S
             for c in range(CHUNKS):
-                nc.scalar.activation(act[h][:, c * CHUNK : (c + 1) * CHUNK], acc[h][c][:], SILU, bias=bias[:, 32 * h : 32 * h + 1])
+                j_cols = slice(c * CHUNK, (c + 1) * CHUNK)
+                if j_cols.start % step == 0:
+                    nc.vector.tensor_copy(
+                        picked[:, j_cols.start : j_cols.start + step],
+                        words[a][:].bitcast(U32).indirect(listed(j_cols.start, step)),
+                    )
+                for h in range(HALVES):
+                    n_cols = slice(h * P, (h + 1) * P)
+                    nc.tensor.matmul_mx(
+                        out=acc[h][c][:],
+                        lhsT=w_codes[a][:, n_cols].bitcast(FP8X4),
+                        lhsT_scale=w_scales[a][:, n_cols],
+                        rhs=picked[:, j_cols].bitcast(FP8X4),
+                        rhs_scale=picked_scales[4 * a : P, j_cols],
+                        start=(a == 0),
+                        stop=(a == PASSES - 1),
+                    )
 
         for h in range(HALVES):
+            act = sbuf("act%d" % h, [P, S], F32)
+            done = sbuf("done%d" % h, [P, S], F32)
+            for c in range(CHUNKS):
+                nc.scalar.activation(act[:, c * CHUNK : (c + 1) * CHUNK], acc[h][c][:], SILU, bias=bias[:, 32 * h : 32 * h + 1])
             first = 0
             for count in PIECES[h]:
                 cols = slice(first, first + count)
-                listed = offsets[:, cols.start // LIST_ROWS : cols.stop // LIST_ROWS]
-                nc.vector.tensor_tensor(done[h][:, cols], resid[h][:].indirect(listed), act[h][:, cols], ADD)
-                nc.sync.dma_start(out[h * P : (h + 1) * P, cols], done[h][:, cols])
+                nc.vector.tensor_tensor(done[:, cols], resid[h][:].indirect(listed(first, count)), act[:, cols], ADD)
+                nc.sync.dma_start(out[h * P : (h + 1) * P, cols], done[:, cols])
                 first = cols.stop

@@ -24,7 +24,7 @@ CHUNKS = S // CHUNK
 LIST_ROWS = 16
 QUADRANTS = 4
 PIECES = ((512, 512, 512), (704, 448, 256, 128))
-SHORT_ROW_BYTES = 4096
+PLANE_ROWS = 4 * PASSES
 
 
 def tile_list_tabres_silu_kernel(tc, tab_words, tab_scales, w, rT, b, offs, out):
@@ -40,44 +40,62 @@ def tile_list_tabres_silu_kernel(tc, tab_words, tab_scales, w, rT, b, offs, out)
             return offsets[:, first // LIST_ROWS : (first + count) // LIST_ROWS]
 
         offsets = held.tile([P, S // LIST_ROWS], U16, name="offsets")
-        scale_rows = sbuf("scale_rows", [P, T // 4], I32, tag="first_gather")
+        scale_rows = sbuf("scale_rows", [P, T // 4], I32)
         bias_rows = sbuf("bias_rows", [P, P], F32)
         w_raw = sbuf("w_raw", [P, PASSES, PACK, M], F32)
         words = [sbuf("words%d" % a, [P, T], I32) for a in range(PASSES)]
-        resid = [sbuf("resid%d" % h, [P, T], F32) for h in range(HALVES)]
 
-        nc.vector.memset(scale_rows[:], 0)
         nc.vector.memset(bias_rows[:], 0.0)
-        for q in range(QUADRANTS):
-            queue = nc.scalar if q == 0 else nc.gpsimd
-            queue.dma_start(
-                scale_rows[32 * q : 32 * q + 4 * PASSES, :],
-                tab_scales[:, 4 * q : 4 * q + 4, :].bitcast(I32),
-            )
-        nc.scalar.dma_start(
-            bias_rows[0:P:32, 0 : HALVES * 32].rearrange("q (h i) -> q h i", h=HALVES),
-            b.rearrange("(h q i) -> q h i", h=HALVES, q=QUADRANTS),
-        )
+        nc.vector.memset(scale_rows[:], 0)
 
+        def load_scales(queue, q):
+            first = 32 * q + PLANE_ROWS * (q % 2)
+            queue.dma_start(scale_rows[first : first + PLANE_ROWS, :], tab_scales[:, 4 * q : 4 * q + 4, :].bitcast(I32))
+
+        def load_bias(q, count):
+            nc.gpsimd.dma_start(
+                bias_rows[32 * q : 32 * (q + count) : 32, 0 : HALVES * 32].rearrange("q (h i) -> q h i", h=HALVES),
+                b.rearrange("(h q i) -> q h i", h=HALVES, q=QUADRANTS)[q : q + count],
+            )
+
+        load_scales(nc.scalar, 0)
+        load_bias(0, 3)
+        load_scales(nc.gpsimd, 1)
+        load_bias(3, 1)
+        load_scales(nc.gpsimd, 2)
+        load_scales(nc.gpsimd, 3)
+
+        def load_words(a):
+            nc.sync.dma_start(words[a][:], tab_words[a].rearrange("p t i -> p (t i)").bitcast(I32))
+
+        load_words(0)
         nc.sync.dma_start(offsets[:], offs)
         nc.sync.dma_start(
             w_raw[:].rearrange("p a j n -> p a (j n)"),
             w.rearrange("(a p j) n -> p a (j n)", a=PASSES, j=PACK),
         )
-        for a in range(PASSES):
-            rows = tab_words[a].rearrange("p t i -> p (t i)").bitcast(I32)
-            nc.sync.dma_start(words[a][:], rows, max_dma_last_dim=SHORT_ROW_BYTES if a == 0 else None)
-        for h in range(HALVES):
-            nc.sync.dma_start(resid[h][:], rT[h * P : (h + 1) * P, :])
+        load_words(1)
+        load_words(2)
 
+        picked = [sbuf("picked%d" % a, [P, S], U32) for a in range(PASSES)]
+
+        def gather_words(a, first, count):
+            nc.vector.tensor_copy(picked[a][:, first : first + count], words[a][:].bitcast(U32).indirect(listed(first, count)))
+
+        gather_words(0, 0, S)
         picked_scales = sbuf("picked_scales", [P, S], U8)
         nc.vector.tensor_copy(picked_scales[:], scale_rows[:].bitcast(U8).indirect(offsets[:]))
-        bias = sbuf("bias", [P, P], F32)
-        nc.vector.transpose(bias[:], bias_rows[:])
+        planes = sbuf("planes", [P, S], U8)
+        nc.vector.tensor_copy(planes[:].bitcast(I32), picked_scales[:].bitcast(I32))
+        for q in range(1, QUADRANTS, 2):
+            nc.sync.dma_start(
+                planes[32 * q : 32 * q + PLANE_ROWS, :].bitcast(I32),
+                picked_scales[32 * q + PLANE_ROWS : 32 * q + 2 * PLANE_ROWS, :].bitcast(I32),
+            )
 
         w_codes, w_scales = [], []
         for a in range(PASSES):
-            rounded = sbuf("w_bf%d" % a, [P, M, PACK], BF16)
+            rounded = sbuf("w_bf%d" % a, [P, M, PACK], BF16, tag="resid%d" % a)
             nc.scalar.copy(rounded[:], w_raw[:, a].rearrange("p j n -> p n j"))
             w_codes.append(sbuf("w_codes%d" % a, [P, M], U32))
             w_scales.append(sbuf("w_scales%d" % a, [P, M], U8))
@@ -86,35 +104,33 @@ def tile_list_tabres_silu_kernel(tc, tab_words, tab_scales, w, rT, b, offs, out)
                 scales=w_scales[a][:],
                 in_=rounded[:].rearrange("p n j -> p (n j)"),
             )
-
-        acc = [[psum.tile([P, CHUNK], F32, name="acc%d_%d" % (h, c)) for c in range(CHUNKS)] for h in range(HALVES)]
-        for a in range(PASSES):
-            picked = sbuf("picked%d" % a, [P, S], U32, tag="first_gather" if a == 0 else None)
-            step = CHUNK if a == PASSES - 1 else S
-            for c in range(CHUNKS):
-                j_cols = slice(c * CHUNK, (c + 1) * CHUNK)
-                if j_cols.start % step == 0:
-                    nc.vector.tensor_copy(
-                        picked[:, j_cols.start : j_cols.start + step],
-                        words[a][:].bitcast(U32).indirect(listed(j_cols.start, step)),
-                    )
-                for h in range(HALVES):
-                    n_cols = slice(h * P, (h + 1) * P)
-                    nc.tensor.matmul_mx(
-                        out=acc[h][c][:],
-                        lhsT=w_codes[a][:, n_cols].bitcast(FP8X4),
-                        lhsT_scale=w_scales[a][:, n_cols],
-                        rhs=picked[:, j_cols].bitcast(FP8X4),
-                        rhs_scale=picked_scales[4 * a : P, j_cols],
-                        start=(a == 0),
-                        stop=(a == PASSES - 1),
-                    )
+        resid = [sbuf("resid%d" % h, [P, T], F32) for h in range(HALVES)]
+        for h in range(HALVES):
+            nc.sync.dma_start(resid[h][:], rT[h * P : (h + 1) * P, :])
+        gather_words(1, 0, S)
+        bias = sbuf("bias", [P, P], F32, tag="words1")
+        nc.vector.transpose(bias[:], bias_rows[:])
+        for c in range(CHUNKS):
+            gather_words(2, c * CHUNK, CHUNK)
 
         for h in range(HALVES):
+            n_cols = slice(h * P, (h + 1) * P)
             act = sbuf("act%d" % h, [P, S], F32)
             done = sbuf("done%d" % h, [P, S], F32)
             for c in range(CHUNKS):
-                nc.scalar.activation(act[:, c * CHUNK : (c + 1) * CHUNK], acc[h][c][:], SILU, bias=bias[:, 32 * h : 32 * h + 1])
+                j_cols = slice(c * CHUNK, (c + 1) * CHUNK)
+                acc = psum.tile([P, CHUNK], F32, name="acc%d_%d" % (h, c))
+                for a in range(PASSES):
+                    nc.tensor.matmul_mx(
+                        out=acc[:],
+                        lhsT=w_codes[a][:, n_cols].bitcast(FP8X4),
+                        lhsT_scale=w_scales[a][:, n_cols],
+                        rhs=picked[a][:, j_cols].bitcast(FP8X4),
+                        rhs_scale=planes[4 * a : P, j_cols],
+                        start=(a == 0),
+                        stop=(a == PASSES - 1),
+                    )
+                nc.scalar.activation(act[:, j_cols], acc[:], SILU, bias=bias[:, 32 * h : 32 * h + 1])
             first = 0
             for count in PIECES[h]:
                 cols = slice(first, first + count)

@@ -66,7 +66,8 @@ def tile_list_tabres_silu_kernel(tc, tab_words, tab_scales, w, rT, b, offs, out)
         load_scales(nc.gpsimd, 3)
 
         def load_words(a):
-            nc.sync.dma_start(words[a][:], tab_words[a].rearrange("p t i -> p (t i)").bitcast(I32))
+            rows = tab_words[a].rearrange("p t i -> p (t i)").bitcast(I32)
+            nc.sync.dma_start(words[a][:], rows, max_dma_last_dim=4096 if a == 1 else None)
 
         load_words(0)
         nc.sync.dma_start(offsets[:], offs)

@@ -45,25 +45,25 @@ def tile_list_tabres_silu_kernel(tc, tab_words, tab_scales, w, rT, b, offs, out)
         w_raw = sbuf("w_raw", [P, PASSES, PACK, M], F32)
         words = [sbuf("words%d" % a, [P, T], I32) for a in range(PASSES)]
 
-        nc.vector.memset(bias_rows[:], 0.0)
         nc.vector.memset(scale_rows[:], 0)
+        nc.vector.memset(bias_rows[:], 0.0)
 
-        def load_scales(queue, q):
+        def load_scales(q):
             first = 32 * q + PLANE_ROWS * (q % 2)
-            queue.dma_start(scale_rows[first : first + PLANE_ROWS, :], tab_scales[:, 4 * q : 4 * q + 4, :].bitcast(I32))
+            nc.gpsimd.dma_start(scale_rows[first : first + PLANE_ROWS, :], tab_scales[:, 4 * q : 4 * q + 4, :].bitcast(I32))
 
-        def load_bias(q, count):
-            nc.gpsimd.dma_start(
-                bias_rows[32 * q : 32 * (q + count) : 32, 0 : HALVES * 32].rearrange("q (h i) -> q h i", h=HALVES),
-                b.rearrange("(h q i) -> q h i", h=HALVES, q=QUADRANTS)[q : q + count],
+        def load_bias(queue, q):
+            queue.dma_start(
+                bias_rows[32 * q : 32 * q + 64 : 32, 0 : HALVES * 32].rearrange("q (h i) -> q h i", h=HALVES),
+                b.rearrange("(h q i) -> q h i", h=HALVES, q=QUADRANTS)[q : q + 2],
             )
 
-        load_scales(nc.scalar, 0)
-        load_bias(0, 3)
-        load_scales(nc.gpsimd, 1)
-        load_bias(3, 1)
-        load_scales(nc.gpsimd, 2)
-        load_scales(nc.gpsimd, 3)
+        load_bias(nc.scalar, 0)
+        load_scales(0)
+        load_scales(1)
+        load_bias(nc.gpsimd, 2)
+        load_scales(2)
+        load_scales(3)
 
         def load_words(a):
             rows = tab_words[a].rearrange("p t i -> p (t i)").bitcast(I32)

@@ -24,7 +24,6 @@ CHUNKS = S // CHUNK
 LIST_ROWS = 16
 QUADRANTS = 4
 PIECES = ((512, 512, 512), (704, 448, 256, 128))
-PLANE_ROWS = 4 * PASSES
 
 
 def tile_list_tabres_silu_kernel(tc, tab_words, tab_scales, w, rT, b, offs, out):
@@ -45,25 +44,23 @@ def tile_list_tabres_silu_kernel(tc, tab_words, tab_scales, w, rT, b, offs, out)
         w_raw = sbuf("w_raw", [P, PASSES, PACK, M], F32)
         words = [sbuf("words%d" % a, [P, T], I32) for a in range(PASSES)]
 
-        nc.vector.memset(scale_rows[:], 0)
         nc.vector.memset(bias_rows[:], 0.0)
+        for partitions in (slice(64, P), slice(32, 64)):
+            nc.vector.memset(scale_rows[partitions, 1:], 0)
+            nc.vector.memset(scale_rows[partitions, 0:1], 0)
 
-        def load_scales(q):
-            first = 32 * q + PLANE_ROWS * (q % 2)
-            nc.gpsimd.dma_start(scale_rows[first : first + PLANE_ROWS, :], tab_scales[:, 4 * q : 4 * q + 4, :].bitcast(I32))
+        def load_scales(partitions, rows, piece=None):
+            nc.gpsimd.dma_start(scale_rows[partitions, :], rows.bitcast(I32), max_dma_last_dim=piece)
 
-        def load_bias(queue, q):
-            queue.dma_start(
-                bias_rows[32 * q : 32 * q + 64 : 32, 0 : HALVES * 32].rearrange("q (h i) -> q h i", h=HALVES),
-                b.rearrange("(h q i) -> q h i", h=HALVES, q=QUADRANTS)[q : q + 2],
-            )
-
-        load_bias(nc.scalar, 0)
-        load_scales(0)
-        load_scales(1)
-        load_bias(nc.gpsimd, 2)
-        load_scales(2)
-        load_scales(3)
+        nc.scalar.dma_start(
+            bias_rows[0:P:32, 0 : HALVES * 32].rearrange("q (h i) -> q h i", h=HALVES),
+            b.rearrange("(h q i) -> q h i", h=HALVES, q=QUADRANTS),
+        )
+        load_scales(slice(0, 12), tab_scales[:, 0:4, :])
+        load_scales(slice(12, 24), tab_scales[:, 4:8, :])
+        load_scales(slice(24, 32), tab_scales[0:2, 12:16, :])
+        load_scales(slice(64, 76), tab_scales[:, 8:12, :])
+        load_scales(slice(76, 92, 4), tab_scales[2, 12:16, :], T // 2)
 
         def load_words(a):
             rows = tab_words[a].rearrange("p t i -> p (t i)").bitcast(I32)
@@ -88,11 +85,8 @@ def tile_list_tabres_silu_kernel(tc, tab_words, tab_scales, w, rT, b, offs, out)
         nc.vector.tensor_copy(picked_scales[:], scale_rows[:].bitcast(U8).indirect(offsets[:]))
         planes = sbuf("planes", [P, S], U8)
         nc.vector.tensor_copy(planes[:].bitcast(I32), picked_scales[:].bitcast(I32))
-        for q in range(1, QUADRANTS, 2):
-            nc.sync.dma_start(
-                planes[32 * q : 32 * q + PLANE_ROWS, :].bitcast(I32),
-                picked_scales[32 * q + PLANE_ROWS : 32 * q + 2 * PLANE_ROWS, :].bitcast(I32),
-            )
+        for home, staged in ((slice(32, 44), slice(12, 24)), (slice(96, 104), slice(24, 32)), (slice(104, 108), slice(76, 92, 4))):
+            nc.sync.dma_start(planes[home, :].bitcast(I32), picked_scales[staged, :].bitcast(I32))
 
         w_codes, w_scales = [], []
         for a in range(PASSES):

@@ -64,7 +64,7 @@ def tile_list_tabres_silu_kernel(tc, tab_words, tab_scales, w, rT, b, offs, out)
 
         def load_words(a):
             rows = tab_words[a].rearrange("p t i -> p (t i)").bitcast(I32)
-            nc.sync.dma_start(words[a][:], rows, max_dma_last_dim=4096 if a == 1 else None)
+            nc.sync.dma_start(words[a][:], rows)
 
         load_words(0)
         nc.sync.dma_start(offsets[:], offs)

@@ -130,5 +130,8 @@ def tile_list_tabres_silu_kernel(tc, tab_words, tab_scales, w, rT, b, offs, out)
             for count in PIECES[h]:
                 cols = slice(first, first + count)
                 nc.vector.tensor_tensor(done[:, cols], resid[h][:].indirect(listed(first, count)), act[:, cols], ADD)
-                nc.sync.dma_start(out[h * P : (h + 1) * P, cols], done[:, cols])
+                if h == 1:
+                    nc.sync.dma_start(out[h * P : (h + 1) * P, cols], done[:, cols])
                 first = cols.stop
+            if h == 0:
+                nc.sync.dma_start(out[0:P, :], done[:])

@@ -23,7 +23,7 @@ CHUNK = 512
 CHUNKS = S // CHUNK
 LIST_ROWS = 16
 QUADRANTS = 4
-PIECES = ((512, 512, 512), (704, 448, 256, 128))
+PIECES = ((512, 256, 256, 256, 256), (704, 448, 256, 128))
 
 
 def tile_list_tabres_silu_kernel(tc, tab_words, tab_scales, w, rT, b, offs, out):

from contextlib import ExitStack

import concourse.mybir as mybir

K, M, T, S = 1536, 256, 4096, 1536
FLOPS = 2 * K * M * S

F32 = mybir.dt.float32
BF16 = mybir.dt.bfloat16
I32 = mybir.dt.int32
U32 = mybir.dt.uint32
U16 = mybir.dt.uint16
U8 = mybir.dt.uint8
FP8X4 = mybir.dt.float8_e4m3fn_x4
SILU = mybir.ActivationFunctionType.Silu
ADD = mybir.AluOpType.add

P = 128
PACK = 4
PASSES = K // (P * PACK)
HALVES = M // P
CHUNK = 512
CHUNKS = S // CHUNK
LIST_ROWS = 16
QUADRANTS = 4
PIECES = ((512, 256, 256, 256, 256), (704, 448, 256, 128))


def tile_list_tabres_silu_kernel(tc, tab_words, tab_scales, w, rT, b, offs, out):
    nc = tc.nc
    with ExitStack() as ctx:
        held = ctx.enter_context(tc.tile_pool(name="held", bufs=1))
        psum = ctx.enter_context(tc.psum_pool(name="psum", bufs=1))

        def sbuf(name, shape, dtype, tag=None):
            return held.tile(shape, dtype, name=name, tag=tag or name, align_bytes=256)

        def listed(first, count):
            return offsets[:, first // LIST_ROWS : (first + count) // LIST_ROWS]

        offsets = held.tile([P, S // LIST_ROWS], U16, name="offsets")
        scale_rows = sbuf("scale_rows", [P, T // 4], I32)
        bias_rows = sbuf("bias_rows", [P, P], F32)
        w_raw = sbuf("w_raw", [P, PASSES, PACK, M], F32)
        words = [sbuf("words%d" % a, [P, T], I32) for a in range(PASSES)]

        nc.vector.memset(bias_rows[:], 0.0)
        for partitions in (slice(64, P), slice(32, 64)):
            nc.vector.memset(scale_rows[partitions, 1:], 0)
            nc.vector.memset(scale_rows[partitions, 0:1], 0)

        def load_scales(partitions, rows, piece=None):
            nc.gpsimd.dma_start(scale_rows[partitions, :], rows.bitcast(I32), max_dma_last_dim=piece)

        nc.scalar.dma_start(
            bias_rows[0:P:32, 0 : HALVES * 32].rearrange("q (h i) -> q h i", h=HALVES),
            b.rearrange("(h q i) -> q h i", h=HALVES, q=QUADRANTS),
        )
        load_scales(slice(0, 12), tab_scales[:, 0:4, :])
        load_scales(slice(12, 24), tab_scales[:, 4:8, :])
        load_scales(slice(24, 32), tab_scales[0:2, 12:16, :])
        load_scales(slice(64, 76), tab_scales[:, 8:12, :])
        load_scales(slice(76, 92, 4), tab_scales[2, 12:16, :], T // 2)

        def load_words(a):
            rows = tab_words[a].rearrange("p t i -> p (t i)").bitcast(I32)
            nc.sync.dma_start(words[a][:], rows)

        load_words(0)
        nc.sync.dma_start(offsets[:], offs)
        nc.sync.dma_start(
            w_raw[:].rearrange("p a j n -> p a (j n)"),
            w.rearrange("(a p j) n -> p a (j n)", a=PASSES, j=PACK),
        )
        load_words(1)
        load_words(2)

        picked = [sbuf("picked%d" % a, [P, S], U32) for a in range(PASSES)]

        def gather_words(a, first, count):
            nc.vector.tensor_copy(picked[a][:, first : first + count], words[a][:].bitcast(U32).indirect(listed(first, count)))

        gather_words(0, 0, S)
        picked_scales = sbuf("picked_scales", [P, S], U8)
        nc.vector.tensor_copy(picked_scales[:], scale_rows[:].bitcast(U8).indirect(offsets[:]))
        planes = sbuf("planes", [P, S], U8)
        nc.vector.tensor_copy(planes[:].bitcast(I32), picked_scales[:].bitcast(I32))
        for home, staged in ((slice(32, 44), slice(12, 24)), (slice(96, 104), slice(24, 32)), (slice(104, 108), slice(76, 92, 4))):
            nc.sync.dma_start(planes[home, :].bitcast(I32), picked_scales[staged, :].bitcast(I32))

        w_codes, w_scales = [], []
        for a in range(PASSES):
            rounded = sbuf("w_bf%d" % a, [P, M, PACK], BF16, tag="resid%d" % a)
            nc.scalar.copy(rounded[:], w_raw[:, a].rearrange("p j n -> p n j"))
            w_codes.append(sbuf("w_codes%d" % a, [P, M], U32))
            w_scales.append(sbuf("w_scales%d" % a, [P, M], U8))
            nc.vector.quantize_mx(
                out=w_codes[a][:].bitcast(FP8X4),
                scales=w_scales[a][:],
                in_=rounded[:].rearrange("p n j -> p (n j)"),
            )
        resid = [sbuf("resid%d" % h, [P, T], F32) for h in range(HALVES)]
        for h in range(HALVES):
            nc.sync.dma_start(resid[h][:], rT[h * P : (h + 1) * P, :])
        gather_words(1, 0, S)
        bias = sbuf("bias", [P, P], F32, tag="words1")
        nc.vector.transpose(bias[:], bias_rows[:])
        for c in range(CHUNKS):
            gather_words(2, c * CHUNK, CHUNK)

        for h in range(HALVES):
            n_cols = slice(h * P, (h + 1) * P)
            act = sbuf("act%d" % h, [P, S], F32)
            done = sbuf("done%d" % h, [P, S], F32)
            for c in range(CHUNKS):
                j_cols = slice(c * CHUNK, (c + 1) * CHUNK)
                acc = psum.tile([P, CHUNK], F32, name="acc%d_%d" % (h, c))
                for a in range(PASSES):
                    nc.tensor.matmul_mx(
                        out=acc[:],
                        lhsT=w_codes[a][:, n_cols].bitcast(FP8X4),
                        lhsT_scale=w_scales[a][:, n_cols],
                        rhs=picked[a][:, j_cols].bitcast(FP8X4),
                        rhs_scale=planes[4 * a : P, j_cols],
                        start=(a == 0),
                        stop=(a == PASSES - 1),
                    )
                nc.scalar.activation(act[:, j_cols], acc[:], SILU, bias=bias[:, 32 * h : 32 * h + 1])
            first = 0
            for count in PIECES[h]:
                cols = slice(first, first + count)
                nc.vector.tensor_tensor(done[:, cols], resid[h][:].indirect(listed(first, count)), act[:, cols], ADD)
                if h == 1:
                    nc.sync.dma_start(out[h * P : (h + 1) * P, cols], done[:, cols])
                first = cols.stop
            if h == 0:
                nc.sync.dma_start(out[0:P, :], done[:])
